import numpy as np
import ml_dtypes


def mxq(x, axis, fmt="e4m3"):
    dtype, down = {"e4m3": (ml_dtypes.float8_e4m3fn, 7), "e5m2": (ml_dtypes.float8_e5m2, 14)}[fmt]
    v = np.moveaxis(np.asarray(x, np.float32).astype(ml_dtypes.bfloat16).astype(np.float64), axis, -1)
    blocks = v.reshape(v.shape[:-1] + (-1, 32))
    amax = np.abs(blocks).max(-1, keepdims=True)
    byte = np.maximum(np.where(amax > 0, np.frexp(amax)[1] - 1 + 127, 0) - down, 1)
    scale = np.exp2(byte - 127.0)
    codes = (blocks / scale).astype(np.float32).astype(dtype).astype(np.float64)
    return np.moveaxis((codes * scale).reshape(v.shape), -1, axis)


WIDE = False


def mx_kscale(k):
    if not WIDE:
        return np.ones(k)
    levels = np.array([10, -10, 5, -5, 0])
    if k % 512:
        return np.exp2(np.random.permutation(np.resize(levels, k // 32))).repeat(32)
    a = np.empty((k // 512, 16))
    for p in range(k // 512):
        a[p, :8] = np.random.permutation(np.resize(levels, 8))
        for g in range(8):
            far = levels[np.abs(levels - a[p, g]) >= 10]
            a[p, g + 8] = far[np.random.randint(len(far))]
    return np.exp2(a.ravel()).repeat(32)


def f64(x):
    return np.asarray(x).astype(np.float64)


def striped(idx):
    return np.tile(idx.reshape(-1, 16).T, (8, 1)).astype(np.uint16)


def unstriped(offs):
    return offs[:16].T.reshape(-1).astype(np.int64)


def striped8(idx):
    return np.concatenate([x.reshape(-1, 16).T for x in idx]).astype(np.uint16)


def runs(offs, k):
    lists = np.stack([offs[16 * r : 16 * r + 16].T.reshape(-1) for r in range(8)]).astype(np.int64)
    return lists[np.arange(k) % 512 // 64]


def pack_weight(w):
    k, n = w.shape
    w = f64(np.asarray(w, np.float32).astype(ml_dtypes.bfloat16)).reshape(k // 32, 32, n)
    amax = np.abs(w).max(1)
    byte = np.clip(np.where(amax > 0, np.frexp(amax)[1] - 1 + 127 - 7, 1), 1, 254)
    scaled = (w * np.exp2(127.0 - byte)[:, None, :]).reshape(k, n).astype(np.float32)
    words = np.ascontiguousarray(scaled.reshape(k // 512, 128, 4, n).transpose(0, 1, 3, 2)).astype(ml_dtypes.float8_e4m3fn).view(np.uint8)
    return words, np.ascontiguousarray(byte.astype(np.uint8).reshape(k // 512, 16, n))


def unpack_weight(words, scales):
    g, p, n, _ = words.shape
    vals = np.ascontiguousarray(words).view(ml_dtypes.float8_e4m3fn).astype(np.float64) * np.repeat(np.exp2(scales.astype(np.float64) - 127.0), 8, axis=1)[..., None]
    return vals.transpose(0, 1, 3, 2).reshape(g * 512, n)


K, T, S, N, H = 512, 2048, 512, 512, 512


def setup_inputs():
    n = np.random.standard_normal
    s = mx_kscale(K)[:, None]
    u = mx_kscale(H)
    packed_xT = pack_weight(n((K, T)) * s)
    return {
        "x_words": packed_xT[0],
        "x_scales": packed_xT[1],
        "w1": (n((K, H)) / np.sqrt(K) / s).astype(np.float32),
        "gn": (np.random.uniform(0.5, 1.5, (H, 1)) * u[:, None]).astype(np.float32),
        "w2": (n((H, N)) / np.sqrt(H) / u[:, None]).astype(np.float32),
        "offs": striped(np.random.permutation(T)[:S]),
        "n1": striped8(np.stack([np.random.permutation(S) for _ in range(8)])),
        "n2": striped8(np.stack([np.random.permutation(S) for _ in range(8)])),
        "n3": striped8(np.stack([np.random.permutation(S) for _ in range(8)])),
        "n4": striped8(np.stack([np.random.permutation(S) for _ in range(8)])),
        "n5": striped8(np.stack([np.random.permutation(S) for _ in range(8)])),
    }


def reference(x_words, x_scales, w1, gn, w2, offs, n1, n2, n3, n4, n5):
    xq = unpack_weight(x_words, x_scales)[:, unstriped(offs)]
    y = mxq(f64(w1), 0, "e4m3").T @ xq
    st = y - (y[np.arange(H)[:, None], runs(n1, H)])
    su = np.maximum(st, st[np.arange(H)[:, None], runs(n2, H)])
    z = f64(gn) * (su + 0.5 * (su[np.arange(H)[:, None], runs(n3, H)]))
    h = mxq(f64(w2), 0, "e4m3").T @ mxq(z, 0, "e4m3")
    return (h * (h[np.arange(N)[:, None], runs(n4, N)])) * (np.tanh(h[np.arange(N)[:, None], runs(n5, N)]))

@@ -1,0 +1,160 @@
+from contextlib import ExitStack
+
+import concourse.mybir as mybir
+
+F32 = mybir.dt.float32
+BF16 = mybir.dt.bfloat16
+I32 = mybir.dt.int32
+U32 = mybir.dt.uint32
+U16 = mybir.dt.uint16
+U8 = mybir.dt.uint8
+FP8X4 = mybir.dt.float8_e4m3fn_x4
+ALU = mybir.AluOpType
+ACT = mybir.ActivationFunctionType
+
+P = 128
+PACK = 4
+T = 2048
+S = 512
+HALF = S // 2
+WIN = 2 * S
+FLOPS = 2 * 2 * 512 * 512 * 512
+
+
+def tile_picked_laythreecube_none_p_kernel(tc, x_words, x_scales, w1, gn, w2, offs, n1, n2, n3, n4, n5, out):
+    nc = tc.nc
+    with ExitStack() as ctx:
+        held = ctx.enter_context(tc.tile_pool(name="held", bufs=1))
+        psum = ctx.enter_context(tc.psum_pool(name="psum", bufs=1))
+
+        def load_list(src, name):
+            tile = held.tile([P, S // 16], U16, name=name)
+            nc.sync.dma_start(tile[:], src)
+            return tile
+
+        x_scale_table = held.tile([P, T], U8, align_bytes=64)
+        nc.vector.memset(x_scale_table[:].bitcast(I32), 0)
+        offs_sb = load_list(offs, "offs_sb")
+        n1_sb = load_list(n1, "n1_sb")
+        n2_sb = load_list(n2, "n2_sb")
+        n3_sb = load_list(n3, "n3_sb")
+        for r in range(4):
+            nc.scalar.dma_start(out=x_scale_table[r:P:32, :].bitcast(I32), in_=x_scales[0, r:16:4, :].bitcast(I32))
+        w1_raw = held.tile([P, PACK, S], F32, tag="w_raw")
+        nc.sync.dma_start(out=w1_raw[:], in_=w1.rearrange("(p j) c -> p j c", j=PACK))
+        x_word_table = held.tile([P, T], I32, align_bytes=64)
+        nc.sync.dma_start(out=x_word_table[:], in_=x_words[0].rearrange("p n t -> p (n t)").bitcast(I32))
+        n4_sb = load_list(n4, "n4_sb")
+        n5_sb = load_list(n5, "n5_sb")
+        gain = held.tile([P, PACK], F32)
+        nc.gpsimd.dma_start(out=gain[:], in_=gn.rearrange("(p t) o -> p (t o)", t=PACK))
+
+        win_a = [held.tile([P, WIN], F32, name="win_a%d" % t) for t in range(PACK)]
+        win_b = [held.tile([P, WIN], F32, name="win_b%d" % t) for t in range(PACK)]
+        for t in range(PACK):
+            nc.vector.memset(win_a[t][:, S:WIN], 0.0)
+            nc.vector.memset(win_b[t][:, S:WIN], 0.0)
+            if t == 0:
+                warm = held.tile([P, 1], F32)
+                nc.scalar.activation(warm[:], win_a[0][:, S : S + 1], ACT.Sigmoid)
+
+        x_scale = held.tile([P, S], U8, align_bytes=64)
+        nc.vector.tensor_copy(x_scale[:], x_scale_table[:].indirect(offs_sb[:]))
+
+        w1_codes = held.tile([P, S], U32, align_bytes=64)
+        w1_scale = held.tile([P, S], U8, align_bytes=64)
+        w1_dealt = w1_raw[:].rearrange("p j (m t) -> p m j t", t=PACK)
+        for u in range(2):
+            w1_bf = held.tile([P, 2 * S], BF16, align_bytes=64, name="w1_bf%d" % u)
+            dst = w1_bf[:].rearrange("p (t m j) -> p m j t", t=2, j=PACK)
+            src = w1_dealt[:, :, :, 2 * u : 2 * u + 2]
+            if u == 0:
+                nc.vector.tensor_copy(dst, src)
+            else:
+                nc.scalar.copy(dst, src)
+            cols = slice(u * HALF, (u + 1) * HALF)
+            nc.vector.quantize_mx(out=w1_codes[:, cols].bitcast(FP8X4), scales=w1_scale[:, cols], in_=w1_bf[:])
+
+        x_codes = held.tile([P, S], U32, align_bytes=64)
+        nc.vector.tensor_copy(x_codes[:], x_word_table[:].bitcast(U32).indirect(offs_sb[:]))
+
+        half_gain = held.tile([P, PACK], F32)
+        nc.vector.tensor_scalar(half_gain[:], gain[:], 0.5, None, ALU.mult)
+
+        banks = []
+        for t in range(PACK):
+            cols = slice(t * P, (t + 1) * P)
+            acc = psum.tile([P, S], F32, name="y_acc%d" % t)
+            nc.tensor.matmul_mx(out=acc[:], lhsT=w1_codes[:, cols].bitcast(FP8X4), lhsT_scale=w1_scale[:, cols],
+                                rhs=x_codes[:].bitcast(FP8X4), rhs_scale=x_scale[:], start=True, stop=True)
+            banks.append(acc)
+
+        plain = [held.tile([P, S], F32, name="plain%d" % t) for t in range(PACK)]
+        su = [held.tile([P, S], F32, name="su%d" % t) for t in range(PACK)]
+
+        def first_step(t):
+            nc.scalar.activation(win_a[t][:, 0:S], banks[t][:], ACT.Copy, scale=-1.0)
+            if t == 0:
+                nc.vector.tensor_scalar(plain[t][:], win_a[t][:, 0:S], -1.0, None, ALU.mult)
+            else:
+                nc.scalar.copy(plain[t][:], banks[t][:])
+            nc.vector.tensor_tensor(win_b[t][:, 0:S], win_a[t][:].indirect(n1_sb[:]), plain[t][:], ALU.add)
+
+        def second_step(t):
+            nc.vector.tensor_copy(su[t][:], win_b[t][:].indirect(n2_sb[:]))
+
+        def third_step(t):
+            nc.vector.tensor_tensor(su[t][:], su[t][:], win_b[t][:, 0:S], ALU.max)
+            nc.scalar.activation(win_a[t][:, 0:S], su[t][:], ACT.Copy, scale=half_gain[:, t : t + 1])
+            nc.scalar.activation(plain[t][:], su[t][:], ACT.Copy, scale=gain[:, t : t + 1])
+
+        for step in range(PACK + 2):
+            if step < PACK:
+                first_step(step)
+            if 0 <= step - 2 < PACK:
+                third_step(step - 2)
+            if 0 <= step - 1 < PACK:
+                second_step(step - 1)
+
+        w2_raw = held.tile([P, PACK, S], F32, tag="w_raw")
+        nc.sync.dma_start(out=w2_raw[:], in_=w2.rearrange("(p j) c -> p j c", j=PACK))
+        w2_bf = held.tile([P, PACK * S], BF16, align_bytes=64)
+        nc.scalar.copy(w2_bf[:].rearrange("p (t m j) -> p m j t", t=PACK, j=PACK),
+                       w2_raw[:].rearrange("p j (m t) -> p m j t", t=PACK))
+        w2_codes = held.tile([P, S], U32, align_bytes=64)
+        w2_scale = held.tile([P, S], U8, align_bytes=64)
+        nc.vector.quantize_mx(out=w2_codes[:].bitcast(FP8X4), scales=w2_scale[:], in_=w2_bf[:])
+
+        h_acc = [psum.tile([P, S], F32, name="h_acc%d" % t) for t in range(PACK)]
+        for u in range(2):
+            cols = slice(u * HALF, (u + 1) * HALF)
+            z = held.tile([P, PACK, HALF], F32, name="z%d" % u)
+            for t in range(PACK):
+                nc.vector.tensor_tensor(z[:, t, :], win_a[t][:].indirect(n3_sb[:, 16 * u : 16 * (u + 1)]),
+                                        plain[t][:, cols], ALU.add)
+            z_bf = held.tile([P, PACK * HALF], BF16, align_bytes=64, name="z_bf%d" % u)
+            dst = z_bf[:].rearrange("p (c i t) -> p c t i", i=4, t=PACK)
+            src = z[:].rearrange("p t (c i) -> p c t i", i=4)
+            if u == 0:
+                nc.scalar.copy(dst, src)
+            else:
+                nc.vector.tensor_copy(dst, src)
+            z_codes = held.tile([P, HALF], U32, align_bytes=64, name="z_codes%d" % u)
+            z_scale = held.tile([P, HALF], U8, align_bytes=64, name="z_scale%d" % u)
+            nc.vector.quantize_mx(out=z_codes[:].bitcast(FP8X4), scales=z_scale[:], in_=z_bf[:])
+            for t in range(PACK):
+                wcols = slice(t * P, (t + 1) * P)
+                nc.tensor.matmul_mx(out=h_acc[t][:, cols], lhsT=w2_codes[:, wcols].bitcast(FP8X4), lhsT_scale=w2_scale[:, wcols],
+                                    rhs=z_codes[:].bitcast(FP8X4), rhs_scale=z_scale[:], start=True, stop=True)
+
+        out_dealt = out.rearrange("(p t) j -> p t j", t=PACK)
+        for t in range(PACK):
+            if t == 1:
+                nc.vector.tensor_scalar(win_b[t][:, 0:S], h_acc[t][:], 2.0, None, ALU.mult)
+            else:
+                nc.scalar.activation(win_b[t][:, 0:S], h_acc[t][:], ACT.Copy, scale=2.0)
+            nc.scalar.activation(su[t][:], win_b[t][:].indirect(n5_sb[:]), ACT.Sigmoid)
+            nc.vector.scalar_tensor_tensor(plain[t][:], su[t][:], -0.5, h_acc[t][:], ALU.add, ALU.mult)
+            result = held.tile([P, S], F32, name="result%d" % t)
+            nc.vector.tensor_tensor(result[:], win_b[t][:].indirect(n4_sb[:]), plain[t][:], ALU.mult)
+            nc.sync.dma_start(out=out_dealt[:, t, :], in_=result[:])

@@ -34,6 +34,8 @@ def tile_picked_laythreecube_none_p_kernel(tc, x_words, x_scales, w1, gn, w2, of
 
         x_scale_table = held.tile([P, T], U8, align_bytes=64)
         nc.vector.memset(x_scale_table[:].bitcast(I32), 0)
+        gain = held.tile([P, PACK], F32)
+        nc.scalar.dma_start(out=gain[:], in_=gn.rearrange("(p t) o -> p (t o)", t=PACK))
         offs_sb = load_list(offs, "offs_sb")
         n1_sb = load_list(n1, "n1_sb")
         n2_sb = load_list(n2, "n2_sb")
@@ -46,8 +48,6 @@ def tile_picked_laythreecube_none_p_kernel(tc, x_words, x_scales, w1, gn, w2, of
         nc.sync.dma_start(out=x_word_table[:], in_=x_words[0].rearrange("p n t -> p (n t)").bitcast(I32))
         n4_sb = load_list(n4, "n4_sb")
         n5_sb = load_list(n5, "n5_sb")
-        gain = held.tile([P, PACK], F32)
-        nc.gpsimd.dma_start(out=gain[:], in_=gn.rearrange("(p t) o -> p (t o)", t=PACK))
 
         win_a = [held.tile([P, WIN], F32, name="win_a%d" % t) for t in range(PACK)]
         win_b = [held.tile([P, WIN], F32, name="win_b%d" % t) for t in range(PACK)]
@@ -78,9 +78,6 @@ def tile_picked_laythreecube_none_p_kernel(tc, x_words, x_scales, w1, gn, w2, of
         x_codes = held.tile([P, S], U32, align_bytes=64)
         nc.vector.tensor_copy(x_codes[:], x_word_table[:].bitcast(U32).indirect(offs_sb[:]))
 
-        half_gain = held.tile([P, PACK], F32)
-        nc.vector.tensor_scalar(half_gain[:], gain[:], 0.5, None, ALU.mult)
-
         banks = []
         for t in range(PACK):
             cols = slice(t * P, (t + 1) * P)
@@ -89,32 +86,29 @@ def tile_picked_laythreecube_none_p_kernel(tc, x_words, x_scales, w1, gn, w2, of
                                 rhs=x_codes[:].bitcast(FP8X4), rhs_scale=x_scale[:], start=True, stop=True)
             banks.append(acc)
 
-        plain = [held.tile([P, S], F32, name="plain%d" % t) for t in range(PACK)]
+        got = [held.tile([P, S], F32, name="got%d" % t) for t in range(PACK)]
         su = [held.tile([P, S], F32, name="su%d" % t) for t in range(PACK)]
+        gained = [held.tile([P, S], F32, name="gained%d" % t) for t in range(PACK)]
 
         def first_step(t):
-            nc.scalar.activation(win_a[t][:, 0:S], banks[t][:], ACT.Copy, scale=-1.0)
-            if t == 0:
-                nc.vector.tensor_scalar(plain[t][:], win_a[t][:, 0:S], -1.0, None, ALU.mult)
-            else:
-                nc.scalar.copy(plain[t][:], banks[t][:])
-            nc.vector.tensor_tensor(win_b[t][:, 0:S], win_a[t][:].indirect(n1_sb[:]), plain[t][:], ALU.add)
+            nc.scalar.copy(win_a[t][:, 0:S], banks[t][:])
+            nc.vector.tensor_copy(got[t][:], win_a[t][:].indirect(n1_sb[:]))
+            nc.gpsimd.tensor_tensor(win_b[t][:, 0:S], win_a[t][:, 0:S], got[t][:], ALU.subtract)
 
         def second_step(t):
             nc.vector.tensor_copy(su[t][:], win_b[t][:].indirect(n2_sb[:]))
 
         def third_step(t):
             nc.vector.tensor_tensor(su[t][:], su[t][:], win_b[t][:, 0:S], ALU.max)
-            nc.scalar.activation(win_a[t][:, 0:S], su[t][:], ACT.Copy, scale=half_gain[:, t : t + 1])
-            nc.scalar.activation(plain[t][:], su[t][:], ACT.Copy, scale=gain[:, t : t + 1])
+            nc.scalar.activation(gained[t][:], su[t][:], ACT.Copy, scale=gain[:, t : t + 1])
 
         for step in range(PACK + 2):
             if step < PACK:
                 first_step(step)
-            if 0 <= step - 2 < PACK:
-                third_step(step - 2)
             if 0 <= step - 1 < PACK:
                 second_step(step - 1)
+            if 0 <= step - 2 < PACK:
+                third_step(step - 2)
 
         w2_raw = held.tile([P, PACK, S], F32, tag="w_raw")
         nc.sync.dma_start(out=w2_raw[:], in_=w2.rearrange("(p j) c -> p j c", j=PACK))
@@ -130,8 +124,10 @@ def tile_picked_laythreecube_none_p_kernel(tc, x_words, x_scales, w1, gn, w2, of
             cols = slice(u * HALF, (u + 1) * HALF)
             z = held.tile([P, PACK, HALF], F32, name="z%d" % u)
             for t in range(PACK):
-                nc.vector.tensor_tensor(z[:, t, :], win_a[t][:].indirect(n3_sb[:, 16 * u : 16 * (u + 1)]),
-                                        plain[t][:, cols], ALU.add)
+                nc.vector.tensor_scalar(got[t][:, cols], gained[t][:].indirect(n3_sb[:, 16 * u : 16 * (u + 1)]),
+                                        0.5, 0.0, ALU.mult, ALU.add)
+                adder = nc.vector if (u, t) == (1, PACK - 1) else nc.gpsimd
+                adder.tensor_tensor(z[:, t, :], got[t][:, cols], gained[t][:, cols], ALU.add)
             z_bf = held.tile([P, PACK * HALF], BF16, align_bytes=64, name="z_bf%d" % u)
             dst = z_bf[:].rearrange("p (c i t) -> p c t i", i=4, t=PACK)
             src = z[:].rearrange("p t (c i) -> p c t i", i=4)
@@ -149,12 +145,11 @@ def tile_picked_laythreecube_none_p_kernel(tc, x_words, x_scales, w1, gn, w2, of
 
         out_dealt = out.rearrange("(p t) j -> p t j", t=PACK)
         for t in range(PACK):
-            if t == 1:
-                nc.vector.tensor_scalar(win_b[t][:, 0:S], h_acc[t][:], 2.0, None, ALU.mult)
-            else:
-                nc.scalar.activation(win_b[t][:, 0:S], h_acc[t][:], ACT.Copy, scale=2.0)
+            nc.scalar.activation(win_b[t][:, 0:S], h_acc[t][:], ACT.Copy, scale=2.0)
+            nc.vector.tensor_copy(got[t][:], win_b[t][:].indirect(n4_sb[:]))
             nc.scalar.activation(su[t][:], win_b[t][:].indirect(n5_sb[:]), ACT.Sigmoid)
-            nc.vector.scalar_tensor_tensor(plain[t][:], su[t][:], -0.5, h_acc[t][:], ALU.add, ALU.mult)
+            nc.vector.scalar_tensor_tensor(gained[t][:], su[t][:], -0.5, h_acc[t][:], ALU.add, ALU.mult)
             result = held.tile([P, S], F32, name="result%d" % t)
-            nc.vector.tensor_tensor(result[:], win_b[t][:].indirect(n4_sb[:]), plain[t][:], ALU.mult)
+            last = nc.vector if t == PACK - 1 else nc.gpsimd
+            last.tensor_tensor(result[:], got[t][:], gained[t][:], ALU.mult)
             nc.sync.dma_start(out=out_dealt[:, t, :], in_=result[:])

@@ -34,29 +34,33 @@ def tile_picked_laythreecube_none_p_kernel(tc, x_words, x_scales, w1, gn, w2, of
 
         x_scale_table = held.tile([P, T], U8, align_bytes=64)
         nc.vector.memset(x_scale_table[:].bitcast(I32), 0)
-        gain = held.tile([P, PACK], F32)
-        nc.scalar.dma_start(out=gain[:], in_=gn.rearrange("(p t) o -> p (t o)", t=PACK))
+        zero = held.tile([P, 1], F32, tag="w_raw")
+        nc.vector.memset(zero[:], 0.0)
+        warm = held.tile([P, 1], F32, tag="small")
+        nc.scalar.activation(warm[:], zero[:], ACT.Tanh)
         offs_sb = load_list(offs, "offs_sb")
         n1_sb = load_list(n1, "n1_sb")
         n2_sb = load_list(n2, "n2_sb")
         n3_sb = load_list(n3, "n3_sb")
-        for r in range(4):
-            nc.scalar.dma_start(out=x_scale_table[r:P:32, :].bitcast(I32), in_=x_scales[0, r:16:4, :].bitcast(I32))
-        w1_raw = held.tile([P, PACK, S], F32, tag="w_raw")
-        nc.sync.dma_start(out=w1_raw[:], in_=w1.rearrange("(p j) c -> p j c", j=PACK))
         x_word_table = held.tile([P, T], I32, align_bytes=64)
         nc.sync.dma_start(out=x_word_table[:], in_=x_words[0].rearrange("p n t -> p (n t)").bitcast(I32))
+        for r in range(4):
+            nc.sync.dma_start(out=x_scale_table[r:P:32, :].bitcast(I32), in_=x_scales[0, r:16:4, :].bitcast(I32))
         n4_sb = load_list(n4, "n4_sb")
         n5_sb = load_list(n5, "n5_sb")
+        w1_raw = held.tile([P, PACK, S], F32, tag="w_raw")
+        nc.sync.dma_start(out=w1_raw[:], in_=w1.rearrange("(p j) c -> p j c", j=PACK))
+        gain = held.tile([P, PACK], F32, tag="small")
+        nc.sync.dma_start(out=gain[:], in_=gn.rearrange("(p t) o -> p (t o)", t=PACK))
 
         win_a = [held.tile([P, WIN], F32, name="win_a%d" % t) for t in range(PACK)]
         win_b = [held.tile([P, WIN], F32, name="win_b%d" % t) for t in range(PACK)]
         for t in range(PACK):
             nc.vector.memset(win_a[t][:, S:WIN], 0.0)
-            nc.vector.memset(win_b[t][:, S:WIN], 0.0)
-            if t == 0:
-                warm = held.tile([P, 1], F32)
-                nc.scalar.activation(warm[:], win_a[0][:, S : S + 1], ACT.Sigmoid)
+            nc.gpsimd.memset(win_b[t][:, S:WIN], 0.0)
+
+        x_codes = held.tile([P, S], U32, align_bytes=64)
+        nc.vector.tensor_copy(x_codes[:], x_word_table[:].bitcast(U32).indirect(offs_sb[:]))
 
         x_scale = held.tile([P, S], U8, align_bytes=64)
         nc.vector.tensor_copy(x_scale[:], x_scale_table[:].indirect(offs_sb[:]))
@@ -75,32 +79,43 @@ def tile_picked_laythreecube_none_p_kernel(tc, x_words, x_scales, w1, gn, w2, of
             cols = slice(u * HALF, (u + 1) * HALF)
             nc.vector.quantize_mx(out=w1_codes[:, cols].bitcast(FP8X4), scales=w1_scale[:, cols], in_=w1_bf[:])
 
-        x_codes = held.tile([P, S], U32, align_bytes=64)
-        nc.vector.tensor_copy(x_codes[:], x_word_table[:].bitcast(U32).indirect(offs_sb[:]))
+        half_gain = held.tile([P, PACK], F32)
+        nc.vector.tensor_scalar(half_gain[:], gain[:], 0.5, None, ALU.mult)
 
+        def product(acc, w_codes, w_scale, t, codes, scale):
+            wcols = slice(t * P, (t + 1) * P)
+            nc.tensor.matmul_mx(out=acc, lhsT=w_codes[:, wcols].bitcast(FP8X4), lhsT_scale=w_scale[:, wcols],
+                                rhs=codes.bitcast(FP8X4), rhs_scale=scale, start=True, stop=True)
+
+        halves = [slice(0, HALF), slice(HALF, S)]
         banks = []
         for t in range(PACK):
-            cols = slice(t * P, (t + 1) * P)
-            acc = psum.tile([P, S], F32, name="y_acc%d" % t)
-            nc.tensor.matmul_mx(out=acc[:], lhsT=w1_codes[:, cols].bitcast(FP8X4), lhsT_scale=w1_scale[:, cols],
-                                rhs=x_codes[:].bitcast(FP8X4), rhs_scale=x_scale[:], start=True, stop=True)
-            banks.append(acc)
+            parts = []
+            for u, cols in enumerate(halves if t == 0 else [slice(0, S)]):
+                acc = psum.tile([P, cols.stop - cols.start], F32, name="y_acc%d%d" % (t, u), tag="bank%d" % (t + 4 * u))
+                product(acc[:], w1_codes, w1_scale, t, x_codes[:, cols], x_scale[:, cols])
+                parts.append((cols, acc))
+            banks.append(parts)
 
-        got = [held.tile([P, S], F32, name="got%d" % t) for t in range(PACK)]
-        su = [held.tile([P, S], F32, name="su%d" % t) for t in range(PACK)]
+        got = [held.tile([P, S], F32, name="got%d" % t) for t in range(PACK + 1)]
+        rival = [held.tile([P, S], F32, align_bytes=64, name="rival%d" % t, tag="z0" if t == PACK - 2 else "rival%d" % t)
+                 for t in range(PACK)]
         gained = [held.tile([P, S], F32, name="gained%d" % t) for t in range(PACK)]
 
         def first_step(t):
-            nc.scalar.copy(win_a[t][:, 0:S], banks[t][:])
+            for cols, acc in banks[t]:
+                nc.scalar.copy(win_a[t][:, cols], acc[:])
             nc.vector.tensor_copy(got[t][:], win_a[t][:].indirect(n1_sb[:]))
             nc.gpsimd.tensor_tensor(win_b[t][:, 0:S], win_a[t][:, 0:S], got[t][:], ALU.subtract)
 
         def second_step(t):
-            nc.vector.tensor_copy(su[t][:], win_b[t][:].indirect(n2_sb[:]))
+            nc.vector.tensor_copy(rival[t][:], win_b[t][:].indirect(n2_sb[:]))
 
         def third_step(t):
-            nc.vector.tensor_tensor(su[t][:], su[t][:], win_b[t][:, 0:S], ALU.max)
-            nc.scalar.activation(gained[t][:], su[t][:], ACT.Copy, scale=gain[:, t : t + 1])
+            su = got[t + 1]
+            nc.vector.tensor_tensor(su[:], rival[t][:], win_b[t][:, 0:S], ALU.max)
+            nc.scalar.activation(win_a[t][:, 0:S], su[:], ACT.Copy, scale=half_gain[:, t : t + 1])
+            nc.scalar.activation(gained[t][:], su[:], ACT.Copy, scale=gain[:, t : t + 1])
 
         for step in range(PACK + 2):
             if step < PACK:
@@ -113,24 +128,22 @@ def tile_picked_laythreecube_none_p_kernel(tc, x_words, x_scales, w1, gn, w2, of
         w2_raw = held.tile([P, PACK, S], F32, tag="w_raw")
         nc.sync.dma_start(out=w2_raw[:], in_=w2.rearrange("(p j) c -> p j c", j=PACK))
         w2_bf = held.tile([P, PACK * S], BF16, align_bytes=64)
-        nc.scalar.copy(w2_bf[:].rearrange("p (t m j) -> p m j t", t=PACK, j=PACK),
-                       w2_raw[:].rearrange("p j (m t) -> p m j t", t=PACK))
+        for m0 in range(0, P, 32):
+            nc.scalar.copy(w2_bf[:].rearrange("p (t m j) -> p m j t", t=PACK, j=PACK)[:, m0 : m0 + 32],
+                           w2_raw[:].rearrange("p j (m t) -> p m j t", t=PACK)[:, m0 : m0 + 32])
         w2_codes = held.tile([P, S], U32, align_bytes=64)
         w2_scale = held.tile([P, S], U8, align_bytes=64)
         nc.vector.quantize_mx(out=w2_codes[:].bitcast(FP8X4), scales=w2_scale[:], in_=w2_bf[:])
 
-        h_acc = [psum.tile([P, S], F32, name="h_acc%d" % t) for t in range(PACK)]
-        for u in range(2):
-            cols = slice(u * HALF, (u + 1) * HALF)
-            z = held.tile([P, PACK, HALF], F32, name="z%d" % u)
+        z_parts = []
+        for u, cols in enumerate(halves):
+            z = held.tile([P, PACK * HALF], F32, align_bytes=64, name="z%d" % u, tag="z%d" % u)
             for t in range(PACK):
-                nc.vector.tensor_scalar(got[t][:, cols], gained[t][:].indirect(n3_sb[:, 16 * u : 16 * (u + 1)]),
-                                        0.5, 0.0, ALU.mult, ALU.add)
-                adder = nc.vector if (u, t) == (1, PACK - 1) else nc.gpsimd
-                adder.tensor_tensor(z[:, t, :], got[t][:, cols], gained[t][:, cols], ALU.add)
+                nc.vector.tensor_tensor(z[:, t * HALF : (t + 1) * HALF],
+                                        win_a[t][:].indirect(n3_sb[:, 16 * u : 16 * (u + 1)]), gained[t][:, cols], ALU.add)
             z_bf = held.tile([P, PACK * HALF], BF16, align_bytes=64, name="z_bf%d" % u)
             dst = z_bf[:].rearrange("p (c i t) -> p c t i", i=4, t=PACK)
-            src = z[:].rearrange("p t (c i) -> p c t i", i=4)
+            src = z[:].rearrange("p (t c i) -> p c t i", t=PACK, i=4)
             if u == 0:
                 nc.scalar.copy(dst, src)
             else:
@@ -138,18 +151,40 @@ def tile_picked_laythreecube_none_p_kernel(tc, x_words, x_scales, w1, gn, w2, of
             z_codes = held.tile([P, HALF], U32, align_bytes=64, name="z_codes%d" % u)
             z_scale = held.tile([P, HALF], U8, align_bytes=64, name="z_scale%d" % u)
             nc.vector.quantize_mx(out=z_codes[:].bitcast(FP8X4), scales=z_scale[:], in_=z_bf[:])
-            for t in range(PACK):
-                wcols = slice(t * P, (t + 1) * P)
-                nc.tensor.matmul_mx(out=h_acc[t][:, cols], lhsT=w2_codes[:, wcols].bitcast(FP8X4), lhsT_scale=w2_scale[:, wcols],
-                                    rhs=z_codes[:].bitcast(FP8X4), rhs_scale=z_scale[:], start=True, stop=True)
+            z_parts.append((z_codes, z_scale))
+
+        h_first = [psum.tile([P, HALF], F32, name="h_first%d" % u, tag="bank%d" % (4 * u)) for u in range(2)]
+        h_acc = [None] + [psum.tile([P, S], F32, name="h_acc%d" % t, tag="bank%d" % (t + 4)) for t in range(1, PACK)]
+        for t in range(PACK):
+            for u, cols in enumerate(halves):
+                product(h_first[u][:] if t == 0 else h_acc[t][:, cols], w2_codes, w2_scale, t, z_parts[u][0][:], z_parts[u][1][:])
 
         out_dealt = out.rearrange("(p t) j -> p t j", t=PACK)
-        for t in range(PACK):
-            nc.scalar.activation(win_b[t][:, 0:S], h_acc[t][:], ACT.Copy, scale=2.0)
-            nc.vector.tensor_copy(got[t][:], win_b[t][:].indirect(n4_sb[:]))
-            nc.scalar.activation(su[t][:], win_b[t][:].indirect(n5_sb[:]), ACT.Sigmoid)
-            nc.vector.scalar_tensor_tensor(gained[t][:], su[t][:], -0.5, h_acc[t][:], ALU.add, ALU.mult)
+
+        def pair_step(t):
+            if t == 0:
+                for u, cols in enumerate(halves):
+                    nc.scalar.copy(win_b[t][:, cols], h_first[u][:])
+                nc.vector.tensor_copy(got[t][:], win_b[t][:, 0:S])
+            else:
+                nc.scalar.copy(win_b[t][:, 0:S], h_acc[t][:])
+                nc.scalar.copy(got[t][:], h_acc[t][:])
+            nc.vector.tensor_tensor(gained[t][:], win_b[t][:].indirect(n4_sb[:]), got[t][:], ALU.mult)
+
+        def tanh_step(t):
+            if t == 0:
+                for u, cols in enumerate(halves):
+                    nc.scalar.activation(win_a[t][:, cols], h_first[u][:], ACT.Tanh)
+            else:
+                nc.scalar.activation(win_a[t][:, 0:S], h_acc[t][:], ACT.Tanh)
             result = held.tile([P, S], F32, name="result%d" % t)
-            last = nc.vector if t == PACK - 1 else nc.gpsimd
-            last.tensor_tensor(result[:], got[t][:], gained[t][:], ALU.mult)
-            nc.sync.dma_start(out=out_dealt[:, t, :], in_=result[:])
+            for cols in halves if t == PACK - 1 else [slice(0, S)]:
+                nc.vector.tensor_tensor(result[:, cols], win_a[t][:].indirect(n5_sb[:, cols.start // 16 : cols.stop // 16]),
+                                        gained[t][:, cols], ALU.mult)
+                nc.sync.dma_start(out=out_dealt[:, t, cols], in_=result[:, cols])
+
+        for step in range(PACK + 1):
+            if step < PACK:
+                pair_step(step)
+            if step > 0:
+                tanh_step(step - 1)

@@ -17,8 +17,14 @@ PACK = 4
 T = 2048
 S = 512
 HALF = S // 2
-WIN = 2 * S
-FLOPS = 2 * 2 * 512 * 512 * 512
+HALVES = (slice(0, HALF), slice(HALF, S))
+WHOLE = slice(0, S)
+WINDOW = 2 * S
+STRIPE = 16
+LINE = 4
+W1_VECTOR_SHARE = (88, 64)
+W2_PIECES = 4
+FLOPS = 2 * 2 * S * S * S
 
 
 def tile_picked_laythreecube_none_p_kernel(tc, x_words, x_scales, w1, gn, w2, offs, n1, n2, n3, n4, n5, out):
@@ -28,16 +34,26 @@ def tile_picked_laythreecube_none_p_kernel(tc, x_words, x_scales, w1, gn, w2, of
         psum = ctx.enter_context(tc.psum_pool(name="psum", bufs=1))
 
         def load_list(src, name):
-            tile = held.tile([P, S // 16], U16, name=name)
+            tile = held.tile([P, S // STRIPE], U16, name=name)
             nc.sync.dma_start(tile[:], src)
             return tile
 
+        def entries(list_tile, cols):
+            return list_tile[:, cols.start // STRIPE : cols.stop // STRIPE]
+
+        def product(acc, w_codes, w_scale, t, codes, scale):
+            slab = slice(t * P, (t + 1) * P)
+            nc.tensor.matmul_mx(out=acc, lhsT=w_codes[:, slab].bitcast(FP8X4), lhsT_scale=w_scale[:, slab],
+                                rhs=codes.bitcast(FP8X4), rhs_scale=scale, start=True, stop=True)
+
         x_scale_table = held.tile([P, T], U8, align_bytes=64)
         nc.vector.memset(x_scale_table[:].bitcast(I32), 0)
+
         zero = held.tile([P, 1], F32, tag="w_raw")
         nc.vector.memset(zero[:], 0.0)
-        warm = held.tile([P, 1], F32, tag="small")
-        nc.scalar.activation(warm[:], zero[:], ACT.Tanh)
+        zero_bias = held.tile([P, 1], F32)
+        nc.scalar.activation(zero_bias[:], zero[:], ACT.Tanh)
+
         offs_sb = load_list(offs, "offs_sb")
         n1_sb = load_list(n1, "n1_sb")
         n2_sb = load_list(n2, "n2_sb")
@@ -50,141 +66,131 @@ def tile_picked_laythreecube_none_p_kernel(tc, x_words, x_scales, w1, gn, w2, of
         n5_sb = load_list(n5, "n5_sb")
         w1_raw = held.tile([P, PACK, S], F32, tag="w_raw")
         nc.sync.dma_start(out=w1_raw[:], in_=w1.rearrange("(p j) c -> p j c", j=PACK))
-        gain = held.tile([P, PACK], F32, tag="small")
-        nc.sync.dma_start(out=gain[:], in_=gn.rearrange("(p t) o -> p (t o)", t=PACK))
 
-        win_a = [held.tile([P, WIN], F32, name="win_a%d" % t) for t in range(PACK)]
-        win_b = [held.tile([P, WIN], F32, name="win_b%d" % t) for t in range(PACK)]
+        first_window = [held.tile([P, WINDOW], F32, name="first_window%d" % t) for t in range(PACK)]
+        second_window = [held.tile([P, WINDOW], F32, name="second_window%d" % t) for t in range(PACK)]
         for t in range(PACK):
-            nc.vector.memset(win_a[t][:, S:WIN], 0.0)
-            nc.gpsimd.memset(win_b[t][:, S:WIN], 0.0)
+            nc.vector.memset(first_window[t][:, S:WINDOW], 0.0)
+            nc.gpsimd.memset(second_window[t][:, S:WINDOW], 0.0)
 
         x_codes = held.tile([P, S], U32, align_bytes=64)
         nc.vector.tensor_copy(x_codes[:], x_word_table[:].bitcast(U32).indirect(offs_sb[:]))
-
         x_scale = held.tile([P, S], U8, align_bytes=64)
         nc.vector.tensor_copy(x_scale[:], x_scale_table[:].indirect(offs_sb[:]))
 
         w1_codes = held.tile([P, S], U32, align_bytes=64)
         w1_scale = held.tile([P, S], U8, align_bytes=64)
         w1_dealt = w1_raw[:].rearrange("p j (m t) -> p m j t", t=PACK)
-        for u in range(2):
-            w1_bf = held.tile([P, 2 * S], BF16, align_bytes=64, name="w1_bf%d" % u)
+        for u, share in enumerate(W1_VECTOR_SHARE):
+            w1_bf = held.tile([P, 2 * S], BF16, align_bytes=64, name="w1_bf%d" % u, tag="w1_bf%d" % u)
             dst = w1_bf[:].rearrange("p (t m j) -> p m j t", t=2, j=PACK)
             src = w1_dealt[:, :, :, 2 * u : 2 * u + 2]
-            if u == 0:
-                nc.vector.tensor_copy(dst, src)
-            else:
-                nc.scalar.copy(dst, src)
-            cols = slice(u * HALF, (u + 1) * HALF)
-            nc.vector.quantize_mx(out=w1_codes[:, cols].bitcast(FP8X4), scales=w1_scale[:, cols], in_=w1_bf[:])
+            nc.vector.tensor_copy(dst[:, 0:share], src[:, 0:share])
+            nc.scalar.copy(dst[:, share:P], src[:, share:P])
+            nc.vector.quantize_mx(out=w1_codes[:, HALVES[u]].bitcast(FP8X4), scales=w1_scale[:, HALVES[u]], in_=w1_bf[:])
 
-        half_gain = held.tile([P, PACK], F32)
-        nc.vector.tensor_scalar(half_gain[:], gain[:], 0.5, None, ALU.mult)
+        gain = held.tile([P, PACK], F32, align_bytes=64, tag="w1_bf1")
+        nc.sync.dma_start(out=gain[:], in_=gn.rearrange("(p t) o -> p (t o)", t=PACK))
 
-        def product(acc, w_codes, w_scale, t, codes, scale):
-            wcols = slice(t * P, (t + 1) * P)
-            nc.tensor.matmul_mx(out=acc, lhsT=w_codes[:, wcols].bitcast(FP8X4), lhsT_scale=w_scale[:, wcols],
-                                rhs=codes.bitcast(FP8X4), rhs_scale=scale, start=True, stop=True)
-
-        halves = [slice(0, HALF), slice(HALF, S)]
-        banks = []
+        y_parts = []
         for t in range(PACK):
             parts = []
-            for u, cols in enumerate(halves if t == 0 else [slice(0, S)]):
-                acc = psum.tile([P, cols.stop - cols.start], F32, name="y_acc%d%d" % (t, u), tag="bank%d" % (t + 4 * u))
+            for u, cols in enumerate(HALVES if t == 0 else (WHOLE,)):
+                acc = psum.tile([P, cols.stop - cols.start], F32, name="y_acc%d%d" % (t, u), tag="bank%d" % (t + PACK * u))
                 product(acc[:], w1_codes, w1_scale, t, x_codes[:, cols], x_scale[:, cols])
                 parts.append((cols, acc))
-            banks.append(parts)
+            y_parts.append(parts)
 
-        got = [held.tile([P, S], F32, name="got%d" % t) for t in range(PACK + 1)]
-        rival = [held.tile([P, S], F32, align_bytes=64, name="rival%d" % t, tag="z0" if t == PACK - 2 else "rival%d" % t)
+        spare = [held.tile([P, S], F32, name="spare%d" % t) for t in range(PACK + 1)]
+        st_n2 = [held.tile([P, S], F32, align_bytes=64, name="st_n2_%d" % t, tag="z0" if t == PACK - 2 else "st_n2_%d" % t)
                  for t in range(PACK)]
-        gained = [held.tile([P, S], F32, name="gained%d" % t) for t in range(PACK)]
+        gained_su = [held.tile([P, S], F32, name="gained_su%d" % t) for t in range(PACK)]
 
-        def first_step(t):
-            for cols, acc in banks[t]:
-                nc.scalar.copy(win_a[t][:, cols], acc[:])
-            nc.vector.tensor_copy(got[t][:], win_a[t][:].indirect(n1_sb[:]))
-            nc.gpsimd.tensor_tensor(win_b[t][:, 0:S], win_a[t][:, 0:S], got[t][:], ALU.subtract)
+        def make_st(t):
+            for cols, acc in y_parts[t]:
+                nc.scalar.copy(first_window[t][:, cols], acc[:])
+            nc.vector.tensor_copy(spare[t][:], first_window[t][:].indirect(n1_sb[:]))
+            nc.gpsimd.tensor_tensor(second_window[t][:, WHOLE], first_window[t][:, WHOLE], spare[t][:], ALU.subtract)
 
-        def second_step(t):
-            nc.vector.tensor_copy(rival[t][:], win_b[t][:].indirect(n2_sb[:]))
+        def fetch_st(t):
+            nc.vector.tensor_copy(st_n2[t][:], second_window[t][:].indirect(n2_sb[:]))
 
-        def third_step(t):
-            su = got[t + 1]
-            nc.vector.tensor_tensor(su[:], rival[t][:], win_b[t][:, 0:S], ALU.max)
-            nc.scalar.activation(win_a[t][:, 0:S], su[:], ACT.Copy, scale=half_gain[:, t : t + 1])
-            nc.scalar.activation(gained[t][:], su[:], ACT.Copy, scale=gain[:, t : t + 1])
+        def make_su(t):
+            su = spare[t + 1]
+            nc.vector.tensor_tensor(su[:], st_n2[t][:], second_window[t][:, WHOLE], ALU.max)
+            nc.scalar.activation(gained_su[t][:], su[:], ACT.Copy, scale=gain[:, t : t + 1])
+            nc.scalar.activation(first_window[t][:, WHOLE], gained_su[t][:], ACT.Copy, scale=0.5)
 
         for step in range(PACK + 2):
             if step < PACK:
-                first_step(step)
-            if 0 <= step - 1 < PACK:
-                second_step(step - 1)
-            if 0 <= step - 2 < PACK:
-                third_step(step - 2)
+                make_st(step)
+            if 1 <= step <= PACK:
+                fetch_st(step - 1)
+            if step >= 2:
+                make_su(step - 2)
 
         w2_raw = held.tile([P, PACK, S], F32, tag="w_raw")
         nc.sync.dma_start(out=w2_raw[:], in_=w2.rearrange("(p j) c -> p j c", j=PACK))
         w2_bf = held.tile([P, PACK * S], BF16, align_bytes=64)
-        for m0 in range(0, P, 32):
-            nc.scalar.copy(w2_bf[:].rearrange("p (t m j) -> p m j t", t=PACK, j=PACK)[:, m0 : m0 + 32],
-                           w2_raw[:].rearrange("p j (m t) -> p m j t", t=PACK)[:, m0 : m0 + 32])
+        for m0 in range(0, P, P // W2_PIECES):
+            piece = slice(m0, m0 + P // W2_PIECES)
+            nc.scalar.copy(w2_bf[:].rearrange("p (t m j) -> p m j t", t=PACK, j=PACK)[:, piece],
+                           w2_raw[:].rearrange("p j (m t) -> p m j t", t=PACK)[:, piece])
         w2_codes = held.tile([P, S], U32, align_bytes=64)
         w2_scale = held.tile([P, S], U8, align_bytes=64)
         nc.vector.quantize_mx(out=w2_codes[:].bitcast(FP8X4), scales=w2_scale[:], in_=w2_bf[:])
 
-        z_parts = []
-        for u, cols in enumerate(halves):
+        z_packed = []
+        for u, cols in enumerate(HALVES):
             z = held.tile([P, PACK * HALF], F32, align_bytes=64, name="z%d" % u, tag="z%d" % u)
             for t in range(PACK):
-                nc.vector.tensor_tensor(z[:, t * HALF : (t + 1) * HALF],
-                                        win_a[t][:].indirect(n3_sb[:, 16 * u : 16 * (u + 1)]), gained[t][:, cols], ALU.add)
+                nc.vector.tensor_tensor(z[:, t * HALF : (t + 1) * HALF], first_window[t][:].indirect(entries(n3_sb, cols)),
+                                        gained_su[t][:, cols], ALU.add)
             z_bf = held.tile([P, PACK * HALF], BF16, align_bytes=64, name="z_bf%d" % u)
-            dst = z_bf[:].rearrange("p (c i t) -> p c t i", i=4, t=PACK)
-            src = z[:].rearrange("p (t c i) -> p c t i", t=PACK, i=4)
-            if u == 0:
-                nc.scalar.copy(dst, src)
-            else:
-                nc.vector.tensor_copy(dst, src)
+            dst = z_bf[:].rearrange("p (c i t) -> p c t i", i=LINE, t=PACK)
+            src = z[:].rearrange("p (t c i) -> p c t i", t=PACK, i=LINE)
+            lines = HALF // LINE
+            nc.scalar.copy(dst[:, 0 : lines // 2], src[:, 0 : lines // 2])
+            nc.vector.tensor_copy(dst[:, lines // 2 : lines], src[:, lines // 2 : lines])
             z_codes = held.tile([P, HALF], U32, align_bytes=64, name="z_codes%d" % u)
             z_scale = held.tile([P, HALF], U8, align_bytes=64, name="z_scale%d" % u)
             nc.vector.quantize_mx(out=z_codes[:].bitcast(FP8X4), scales=z_scale[:], in_=z_bf[:])
-            z_parts.append((z_codes, z_scale))
+            z_packed.append((z_codes, z_scale))
 
-        h_first = [psum.tile([P, HALF], F32, name="h_first%d" % u, tag="bank%d" % (4 * u)) for u in range(2)]
-        h_acc = [None] + [psum.tile([P, S], F32, name="h_acc%d" % t, tag="bank%d" % (t + 4)) for t in range(1, PACK)]
+        h_first = [psum.tile([P, HALF], F32, name="h_first%d" % u, tag="bank%d" % (PACK * u)) for u in range(2)]
+        h_rest = {t: psum.tile([P, S], F32, name="h_rest%d" % t, tag="bank%d" % (t + PACK)) for t in range(1, PACK)}
         for t in range(PACK):
-            for u, cols in enumerate(halves):
-                product(h_first[u][:] if t == 0 else h_acc[t][:, cols], w2_codes, w2_scale, t, z_parts[u][0][:], z_parts[u][1][:])
+            for u, cols in enumerate(HALVES):
+                z_codes, z_scale = z_packed[u]
+                product(h_first[u][:] if t == 0 else h_rest[t][:, cols], w2_codes, w2_scale, t, z_codes[:], z_scale[:])
 
         out_dealt = out.rearrange("(p t) j -> p t j", t=PACK)
+        h_pair = gained_su
 
-        def pair_step(t):
+        def make_pair(t):
             if t == 0:
-                for u, cols in enumerate(halves):
-                    nc.scalar.copy(win_b[t][:, cols], h_first[u][:])
-                nc.vector.tensor_copy(got[t][:], win_b[t][:, 0:S])
+                for u, cols in enumerate(HALVES):
+                    nc.scalar.copy(second_window[t][:, cols], h_first[u][:])
+                    nc.vector.tensor_copy(spare[t][:, cols], second_window[t][:, cols])
             else:
-                nc.scalar.copy(win_b[t][:, 0:S], h_acc[t][:])
-                nc.scalar.copy(got[t][:], h_acc[t][:])
-            nc.vector.tensor_tensor(gained[t][:], win_b[t][:].indirect(n4_sb[:]), got[t][:], ALU.mult)
+                nc.scalar.copy(second_window[t][:, WHOLE], h_rest[t][:])
+                nc.scalar.copy(spare[t][:], h_rest[t][:])
+            nc.vector.tensor_tensor(h_pair[t][:], second_window[t][:].indirect(n4_sb[:]), spare[t][:], ALU.mult)
 
-        def tanh_step(t):
+        def make_out(t):
             if t == 0:
-                for u, cols in enumerate(halves):
-                    nc.scalar.activation(win_a[t][:, cols], h_first[u][:], ACT.Tanh)
+                for u, cols in enumerate(HALVES):
+                    nc.scalar.activation(first_window[t][:, cols], h_first[u][:], ACT.Tanh, bias=zero_bias[:])
             else:
-                nc.scalar.activation(win_a[t][:, 0:S], h_acc[t][:], ACT.Tanh)
+                nc.scalar.activation(first_window[t][:, WHOLE], h_rest[t][:], ACT.Tanh, bias=zero_bias[:])
             result = held.tile([P, S], F32, name="result%d" % t)
-            for cols in halves if t == PACK - 1 else [slice(0, S)]:
-                nc.vector.tensor_tensor(result[:, cols], win_a[t][:].indirect(n5_sb[:, cols.start // 16 : cols.stop // 16]),
-                                        gained[t][:, cols], ALU.mult)
+            for cols in HALVES if t == PACK - 1 else (WHOLE,):
+                nc.vector.tensor_tensor(result[:, cols], first_window[t][:].indirect(entries(n5_sb, cols)),
+                                        h_pair[t][:, cols], ALU.mult)
                 nc.sync.dma_start(out=out_dealt[:, t, cols], in_=result[:, cols])
 
         for step in range(PACK + 1):
             if step < PACK:
-                pair_step(step)
-            if step > 0:
-                tanh_step(step - 1)
+                make_pair(step)
+            if step >= 1:
+                make_out(step - 1)

from contextlib import ExitStack

import concourse.mybir as mybir

F32 = mybir.dt.float32
BF16 = mybir.dt.bfloat16
I32 = mybir.dt.int32
U32 = mybir.dt.uint32
U16 = mybir.dt.uint16
U8 = mybir.dt.uint8
FP8X4 = mybir.dt.float8_e4m3fn_x4
ALU = mybir.AluOpType
ACT = mybir.ActivationFunctionType

P = 128
PACK = 4
T = 2048
S = 512
HALF = S // 2
HALVES = (slice(0, HALF), slice(HALF, S))
WHOLE = slice(0, S)
WINDOW = 2 * S
STRIPE = 16
LINE = 4
W1_VECTOR_SHARE = (88, 64)
W2_PIECES = 4
FLOPS = 2 * 2 * S * S * S


def tile_picked_laythreecube_none_p_kernel(tc, x_words, x_scales, w1, gn, w2, offs, n1, n2, n3, n4, n5, out):
    nc = tc.nc
    with ExitStack() as ctx:
        held = ctx.enter_context(tc.tile_pool(name="held", bufs=1))
        psum = ctx.enter_context(tc.psum_pool(name="psum", bufs=1))

        def load_list(src, name):
            tile = held.tile([P, S // STRIPE], U16, name=name)
            nc.sync.dma_start(tile[:], src)
            return tile

        def entries(list_tile, cols):
            return list_tile[:, cols.start // STRIPE : cols.stop // STRIPE]

        def product(acc, w_codes, w_scale, t, codes, scale):
            slab = slice(t * P, (t + 1) * P)
            nc.tensor.matmul_mx(out=acc, lhsT=w_codes[:, slab].bitcast(FP8X4), lhsT_scale=w_scale[:, slab],
                                rhs=codes.bitcast(FP8X4), rhs_scale=scale, start=True, stop=True)

        x_scale_table = held.tile([P, T], U8, align_bytes=64)
        nc.vector.memset(x_scale_table[:].bitcast(I32), 0)

        zero = held.tile([P, 1], F32, tag="w_raw")
        nc.vector.memset(zero[:], 0.0)
        zero_bias = held.tile([P, 1], F32)
        nc.scalar.activation(zero_bias[:], zero[:], ACT.Tanh)

        offs_sb = load_list(offs, "offs_sb")
        n1_sb = load_list(n1, "n1_sb")
        n2_sb = load_list(n2, "n2_sb")
        n3_sb = load_list(n3, "n3_sb")
        x_word_table = held.tile([P, T], I32, align_bytes=64)
        nc.sync.dma_start(out=x_word_table[:], in_=x_words[0].rearrange("p n t -> p (n t)").bitcast(I32))
        for r in range(4):
            nc.sync.dma_start(out=x_scale_table[r:P:32, :].bitcast(I32), in_=x_scales[0, r:16:4, :].bitcast(I32))
        n4_sb = load_list(n4, "n4_sb")
        n5_sb = load_list(n5, "n5_sb")
        w1_raw = held.tile([P, PACK, S], F32, tag="w_raw")
        nc.sync.dma_start(out=w1_raw[:], in_=w1.rearrange("(p j) c -> p j c", j=PACK))

        first_window = [held.tile([P, WINDOW], F32, name="first_window%d" % t) for t in range(PACK)]
        second_window = [held.tile([P, WINDOW], F32, name="second_window%d" % t) for t in range(PACK)]
        for t in range(PACK):
            nc.vector.memset(first_window[t][:, S:WINDOW], 0.0)
            nc.gpsimd.memset(second_window[t][:, S:WINDOW], 0.0)

        x_codes = held.tile([P, S], U32, align_bytes=64)
        nc.vector.tensor_copy(x_codes[:], x_word_table[:].bitcast(U32).indirect(offs_sb[:]))
        x_scale = held.tile([P, S], U8, align_bytes=64)
        nc.vector.tensor_copy(x_scale[:], x_scale_table[:].indirect(offs_sb[:]))

        w1_codes = held.tile([P, S], U32, align_bytes=64)
        w1_scale = held.tile([P, S], U8, align_bytes=64)
        w1_dealt = w1_raw[:].rearrange("p j (m t) -> p m j t", t=PACK)
        for u, share in enumerate(W1_VECTOR_SHARE):
            w1_bf = held.tile([P, 2 * S], BF16, align_bytes=64, name="w1_bf%d" % u, tag="w1_bf%d" % u)
            dst = w1_bf[:].rearrange("p (t m j) -> p m j t", t=2, j=PACK)
            src = w1_dealt[:, :, :, 2 * u : 2 * u + 2]
            nc.vector.tensor_copy(dst[:, 0:share], src[:, 0:share])
            nc.scalar.copy(dst[:, share:P], src[:, share:P])
            nc.vector.quantize_mx(out=w1_codes[:, HALVES[u]].bitcast(FP8X4), scales=w1_scale[:, HALVES[u]], in_=w1_bf[:])

        gain = held.tile([P, PACK], F32, align_bytes=64, tag="w1_bf1")
        nc.sync.dma_start(out=gain[:], in_=gn.rearrange("(p t) o -> p (t o)", t=PACK))

        y_parts = []
        for t in range(PACK):
            parts = []
            for u, cols in enumerate(HALVES if t == 0 else (WHOLE,)):
                acc = psum.tile([P, cols.stop - cols.start], F32, name="y_acc%d%d" % (t, u), tag="bank%d" % (t + PACK * u))
                product(acc[:], w1_codes, w1_scale, t, x_codes[:, cols], x_scale[:, cols])
                parts.append((cols, acc))
            y_parts.append(parts)

        spare = [held.tile([P, S], F32, name="spare%d" % t) for t in range(PACK + 1)]
        st_n2 = [held.tile([P, S], F32, align_bytes=64, name="st_n2_%d" % t, tag="z0" if t == PACK - 2 else "st_n2_%d" % t)
                 for t in range(PACK)]
        gained_su = [held.tile([P, S], F32, name="gained_su%d" % t) for t in range(PACK)]

        def make_st(t):
            for cols, acc in y_parts[t]:
                nc.scalar.copy(first_window[t][:, cols], acc[:])
            nc.vector.tensor_copy(spare[t][:], first_window[t][:].indirect(n1_sb[:]))
            nc.gpsimd.tensor_tensor(second_window[t][:, WHOLE], first_window[t][:, WHOLE], spare[t][:], ALU.subtract)

        def fetch_st(t):
            nc.vector.tensor_copy(st_n2[t][:], second_window[t][:].indirect(n2_sb[:]))

        def make_su(t):
            su = spare[t + 1]
            nc.vector.tensor_tensor(su[:], st_n2[t][:], second_window[t][:, WHOLE], ALU.max)
            nc.scalar.activation(gained_su[t][:], su[:], ACT.Copy, scale=gain[:, t : t + 1])
            nc.scalar.activation(first_window[t][:, WHOLE], gained_su[t][:], ACT.Copy, scale=0.5)

        for step in range(PACK + 2):
            if step < PACK:
                make_st(step)
            if 1 <= step <= PACK:
                fetch_st(step - 1)
            if step >= 2:
                make_su(step - 2)

        w2_raw = held.tile([P, PACK, S], F32, tag="w_raw")
        nc.sync.dma_start(out=w2_raw[:], in_=w2.rearrange("(p j) c -> p j c", j=PACK))
        w2_bf = held.tile([P, PACK * S], BF16, align_bytes=64)
        for m0 in range(0, P, P // W2_PIECES):
            piece = slice(m0, m0 + P // W2_PIECES)
            nc.scalar.copy(w2_bf[:].rearrange("p (t m j) -> p m j t", t=PACK, j=PACK)[:, piece],
                           w2_raw[:].rearrange("p j (m t) -> p m j t", t=PACK)[:, piece])
        w2_codes = held.tile([P, S], U32, align_bytes=64)
        w2_scale = held.tile([P, S], U8, align_bytes=64)
        nc.vector.quantize_mx(out=w2_codes[:].bitcast(FP8X4), scales=w2_scale[:], in_=w2_bf[:])

        z_packed = []
        for u, cols in enumerate(HALVES):
            z = held.tile([P, PACK * HALF], F32, align_bytes=64, name="z%d" % u, tag="z%d" % u)
            for t in range(PACK):
                nc.vector.tensor_tensor(z[:, t * HALF : (t + 1) * HALF], first_window[t][:].indirect(entries(n3_sb, cols)),
                                        gained_su[t][:, cols], ALU.add)
            z_bf = held.tile([P, PACK * HALF], BF16, align_bytes=64, name="z_bf%d" % u)
            dst = z_bf[:].rearrange("p (c i t) -> p c t i", i=LINE, t=PACK)
            src = z[:].rearrange("p (t c i) -> p c t i", t=PACK, i=LINE)
            lines = HALF // LINE
            nc.scalar.copy(dst[:, 0 : lines // 2], src[:, 0 : lines // 2])
            nc.vector.tensor_copy(dst[:, lines // 2 : lines], src[:, lines // 2 : lines])
            z_codes = held.tile([P, HALF], U32, align_bytes=64, name="z_codes%d" % u)
            z_scale = held.tile([P, HALF], U8, align_bytes=64, name="z_scale%d" % u)
            nc.vector.quantize_mx(out=z_codes[:].bitcast(FP8X4), scales=z_scale[:], in_=z_bf[:])
            z_packed.append((z_codes, z_scale))

        h_first = [psum.tile([P, HALF], F32, name="h_first%d" % u, tag="bank%d" % (PACK * u)) for u in range(2)]
        h_rest = {t: psum.tile([P, S], F32, name="h_rest%d" % t, tag="bank%d" % (t + PACK)) for t in range(1, PACK)}
        for t in range(PACK):
            for u, cols in enumerate(HALVES):
                z_codes, z_scale = z_packed[u]
                product(h_first[u][:] if t == 0 else h_rest[t][:, cols], w2_codes, w2_scale, t, z_codes[:], z_scale[:])

        out_dealt = out.rearrange("(p t) j -> p t j", t=PACK)
        h_pair = gained_su

        def make_pair(t):
            if t == 0:
                for u, cols in enumerate(HALVES):
                    nc.scalar.copy(second_window[t][:, cols], h_first[u][:])
                    nc.vector.tensor_copy(spare[t][:, cols], second_window[t][:, cols])
            else:
                nc.scalar.copy(second_window[t][:, WHOLE], h_rest[t][:])
                nc.scalar.copy(spare[t][:], h_rest[t][:])
            nc.vector.tensor_tensor(h_pair[t][:], second_window[t][:].indirect(n4_sb[:]), spare[t][:], ALU.mult)

        def make_out(t):
            if t == 0:
                for u, cols in enumerate(HALVES):
                    nc.scalar.activation(first_window[t][:, cols], h_first[u][:], ACT.Tanh, bias=zero_bias[:])
            else:
                nc.scalar.activation(first_window[t][:, WHOLE], h_rest[t][:], ACT.Tanh, bias=zero_bias[:])
            result = held.tile([P, S], F32, name="result%d" % t)
            for cols in HALVES if t == PACK - 1 else (WHOLE,):
                nc.vector.tensor_tensor(result[:, cols], first_window[t][:].indirect(entries(n5_sb, cols)),
                                        h_pair[t][:, cols], ALU.mult)
                nc.sync.dma_start(out=out_dealt[:, t, cols], in_=result[:, cols])

        for step in range(PACK + 1):
            if step < PACK:
                make_pair(step)
            if step >= 1:
                make_out(step - 1)
